import numpy as np, ml_dtypes
CORES = [36,164,52,180,100,228,116,244]
N = 8
import mx_ref
BF = ml_dtypes.bfloat16
def gentries(a):
    return np.ascontiguousarray(a.reshape(8, 16, -1).transpose(0, 2, 1)).reshape(8, -1)
def gtable(e):
    e = np.asarray(e); return np.ascontiguousarray(e.reshape(8, -1, 16).transpose(0, 2, 1)).reshape(128, -1).astype(np.int32)
def gcols(t, e):
    v = np.concatenate([t.reshape(8, 16, -1, 4), np.zeros((8, 16, 1, 4), BF)], axis=2)
    return np.ascontiguousarray(np.stack([v[g][:, e[g]] for g in range(8)])).reshape(128, -1)
def tile(rs):
    return np.stack(rs, axis=2).reshape(128, -1).astype(BF)
def pick(q, e):
    c = np.concatenate([q[0].reshape(128, -1, 4), np.zeros((128, 1, 4), np.uint8)], axis=1); s = np.concatenate([q[1], np.ones((16, 1), np.uint8)], axis=1)
    return (np.ascontiguousarray(c[:, e].reshape(128, -1)), np.ascontiguousarray(s[:, e]))
def join(*qs):
    return (np.concatenate([q[0] for q in qs], axis=1), np.concatenate([q[1] for q in qs], axis=1))
def put(q, e, v):
    c, s = q[0].reshape(128, -1, 4).copy(), q[1].copy(); c[:, e] = v[0].reshape(128, -1, 4); s[:, e] = v[1]
    return (c.reshape(128, -1), s)
def pk(c, s):
    return (np.ascontiguousarray(c), mx_ref.live(s))
def emit(q):
    return q[0], q[1]
def packed(v, rng):
    q = [mx_ref.quantize(np.ascontiguousarray(v[r])) for r in range(N)]
    return np.stack([a for a, b in q]), np.stack([mx_ref.plane(b, rng) for a, b in q])
def values_of_codes():
    e, c = np.zeros((128, 128, 4), np.float32), np.zeros((128, 2, 4), np.uint8)
    e[np.arange(128), np.arange(128), 0] = 1
    c[:127, :, 0] = np.arange(256).reshape(2, 128).T[:127]
    return mx_ref.matmul(mx_ref.quantize(e.reshape(128, 512).astype(BF)), (c.reshape(128, 8), np.full((16, 2), 127, np.uint8))).T.reshape(-1).astype(np.float64)
CODE_VALUE, SCALE_VALUE = values_of_codes(), 2.0 ** (np.arange(256) - 127.0)
def decode(q):
    return (CODE_VALUE[q[0]].reshape(16, 8, -1, 4) * SCALE_VALUE[q[1]][:, None, :, None] + 0.0).reshape(128, -1).astype(np.float32)
def f(rng, *shape):
    return mx_ref.flush((rng.standard_normal(shape, dtype=np.float32) * np.exp2(rng.integers(-2, 3, shape[:-1] + (1,)))).astype(BF))
def wide(rng, *shape, cols=0):
    v = rng.standard_normal(shape, dtype=np.float32) * np.exp2(rng.integers(-12, 13, shape)).astype(np.float32)
    if cols: v *= np.repeat(np.exp2(rng.integers(-cols, cols + 1, shape[:-2] + (1, shape[-1] // 4))) * (rng.random(shape[:-2] + (1, shape[-1] // 4)) > 0.0625), 4, axis=-1).astype(np.float32)
    return mx_ref.flush(v.astype(BF))
C, T, R = 288, 2304, 3
def big(v):
    v = v.astype(np.float32)
    v[np.abs(v) < np.float32(2.0 ** -12)] = 0
    return v.astype(BF)
def numbers_of(rng):
    return {"x": big(f(rng, N, 128, 4 * C)), "u": np.array(f(rng, N, 128, 512)), "v": np.array(f(rng, N, 128, 512))}
def lists_of(t):
    return np.stack([gtable(t[r]) for r in range(N)])
def layers(rng, still=[], full=False):
    w = np.zeros((N, 512, 512), np.float32)
    k = rng.random((N, 512, 512))
    k[:, :, np.isin(np.arange(512) // 4 % 16, still)] = 2
    e = np.argpartition(k, 8, axis=2)[:, :, :8]
    a = rng.integers(4, 16, (N, 512, 8)) * 0.25 * rng.choice([-1.0, 1.0], (N, 512, 8))
    if full: a = 4.0 * rng.choice([-1.0, 1.0], (N, 512, 1)) * np.ones((1, 1, 8))
    np.put_along_axis(w, e, a.astype(np.float32), axis=2)
    w[:, np.isin(np.arange(512) % 16, still)] = 0
    return w
def weights(rng, w):
    c, s = packed(np.ascontiguousarray(w.reshape(N, 512, 128, 4).transpose(0, 2, 1, 3)).reshape(N, 128, 2048).astype(BF), rng)
    return {"wc": c, "ws": s}
def setup_inputs(rng):
    return {**numbers_of(rng), "p": lists_of(rng.integers(0, T, (N, 8, C))), **weights(rng, layers(rng))}
def setup_inputs_ties(rng):
    d = numbers_of(rng)
    x = d["x"].reshape(N, 8, 16, C, 4)
    x[:, :, 0] = 0
    x[:, :, 0, :, 0] = rng.integers(0, 3, (N, 8, C)).astype(np.float32).astype(BF)
    u = d["u"].reshape(N, 128, 128, 4)
    u[:, :, ::16] = 0
    o = rng.permutation(N)
    for r in range(N):
        for h in range(0, 128, 16): u[r, h, h, 0] = 0.0 if r == o[0] else -1.0 if r == o[1] else 1.0
    t = rng.integers(0, T, (N, 8, C))
    t[o[:2]] = C * rng.integers(0, 4, (2, 8, C))
    t[o[2]] = rng.integers(0, T)
    t[o[3]] = C * (7 - np.arange(8))[:, None]
    return {"x": x.reshape(N, 128, 4 * C), "u": u.reshape(N, 128, 512), "v": d["v"], "p": lists_of(t), **weights(rng, layers(rng, [0]))}
def setup_inputs_near(rng):
    d = numbers_of(rng)
    x = d["x"].astype(np.float32).reshape(N, 8, 16, C, 4)
    x[:, :, 0] = 0
    x[:, :, 8:] = 0
    u = d["u"].reshape(N, 128, 128, 4)
    u[:, :, ::16] = 0
    t = rng.integers(0, T, (N, 8, C))
    o = rng.permutation(N) % 4
    for r in range(N):
        s = rng.integers(0, 16, (8, C))
        if o[r] == 1:
            s[5:] = np.minimum(s[5:], 12)
            s[5:, 4:9] = [15, 15, 14, 13, 12]
            t[r] = np.minimum(t[r], T - 2)
            t[r, 5, :16] = T - 1
            t[r, 6, :9] = T - 1
            t[r, 7, :7] = T - 1
        if o[r] < 3: x[r, :, 8] = ((s[:, :, None] >> np.arange(4)) & 1) * np.exp2(np.arange(4) - 22.0)
        if o[r] < 2:
            x[r, :, 0, :, 0] = rng.choice([-1.0, 1.0], (8, 1))
            x[r, :, 11, :, 0] = 2.0 ** -10
        if o[r] == 2:
            for g in rng.permutation(8)[:4]: x[r, g, 0, rng.integers(C), 0] = 2.0 ** 26 * rng.choice([-1.0, 1.0])
        if o[r] == 3:
            x[r, :, 10, :, 0] = np.where(s < 8, 1.125 * 2.0 ** -29, 0.0)
            x[r, :, 11, :, 0] = np.where(s < 8, 0.0, 2.0 ** -29)
        k = 1.0 if o[r] == 0 else 2.0 ** -30
        for h in range(0, 128, 16):
            if o[r] < 2:
                u[r, h, h, 0] = k
                u[r, h + 11, h, 0] = k
            if o[r] == 2: u[r, h, h, 0] = 2.0 ** 30
            if o[r] < 3: u[r, h + 8, h] = k
            else:
                u[r, h + 10, h, 0] = 1.125 * k
                u[r, h + 11, h, 0] = 1.25 * k
    return {"x": x.reshape(N, 128, 4 * C).astype(BF), "u": u.reshape(N, 128, 512), "v": d["v"], "p": lists_of(t), **weights(rng, layers(rng, [0, 8, 9, 10, 11, 12, 13, 14, 15]))}
def setup_inputs_fine(rng):
    d = numbers_of(rng)
    x = (1.0 + (2 * rng.integers(0, 64, (N, 8, 2, 8, C, 4)) + 1) * 2.0 ** -7) * np.exp2(-rng.integers(8, 15, (N, 8, 2, 8, C, 4))) * rng.choice([-1.0, 1.0], (N, 8, 2, 8, C, 4))
    np.put_along_axis(x[..., 0], rng.integers(0, 8, (N, 8, 2, 1, C)), 1.96875 * rng.choice([-1.0, 1.0], (N, 8, 2, 1, C)), axis=3)
    x = x * np.exp2(rng.integers(-1, 3, (N, 8, 2, 1, C, 1)))
    return {"x": x.astype(np.float32).reshape(N, 128, 4 * C).astype(BF), "u": d["u"], "v": d["v"], "p": lists_of(rng.integers(0, T, (N, 8, C))), **weights(rng, layers(rng))}
def setup_inputs_ends(rng):
    k = int(rng.integers(0, 2))
    o = np.roll(np.array([2, 3, k, 1 - k])[np.arange(N) % 4], int(rng.integers(0, N)))
    sign = np.array([1.0, -1.0, 1.0, 1.0])
    x = np.zeros((N, 8, 16, C, 4))
    u = np.array(f(rng, N, 128, 512)).reshape(N, 128, 128, 4)
    v = (rng.integers(0, 2, (N, 128, 512)) * 2.0 - 1.0) * 2.0 ** 30
    w = layers(rng, full=True)
    t = np.zeros((N, 8, C), np.int64)
    for r in range(N):
        a = 2.0 ** 26 * rng.choice([1.0, 0.875, 0.75], (8, 1, C, 1))
        if o[r] == 0: x[r] = a
        if o[r] == 1:
            x[r] = -a
            t[r] = T - 1
        if o[r] < 2:
            w[r] = np.abs(w[r]) * (sign[o[r]] * sign[o[r - 1]])
            if o[r - 1] == 3:
                w[r, :, :64] = np.sum(w[r].reshape(512, 8, 64), axis=1)
                w[r, :, 64:] = 0
        if o[r] == 2:
            x[r] = 2.0 ** -30
            w[r] = 0
            t[r] = (T - 1) * rng.integers(0, 2, (8, C))
        if o[r] == 3:
            x[r] = 2.0 ** 26 * rng.choice([-1.0, 1.0], (8, 1, C, 1))
            x[r, 0] = 2.0 ** 26
            t[r] = (T - 1) * (rng.permutation(8) % 2)[:, None]
        h = rng.permutation(6) % 2 * 2.0 - 1.0
        for g in range(8): u[r, :, 16 * g] = 0.0 if g in (0, 7) else (2.0 ** -30 if o[r] == 2 else 2.0 ** 30) * float(h[g - 1])
    v = (np.where(v < 0, -1.0, 1.0) * np.where(rng.permutation(N) % 2, 2.0 ** -30, 2.0 ** 30)[:, None, None]).astype(np.float32).astype(BF)
    return {"x": x.astype(np.float32).reshape(N, 128, 4 * C).astype(BF), "u": u.reshape(N, 128, 512), "v": v.astype(np.float32).astype(BF), "p": lists_of(t), **weights(rng, w)}
def setup_inputs_spread(rng):
    d = setup_inputs(rng)
    d["x"] = big(wide(rng, N, 128, 4 * C, cols=6))
    return d
def check_inputs(d):
    b = []
    for k, most in (("x", 2.0 ** 26), ("u", 2.0 ** 30), ("v", 2.0 ** 30)):
        a = np.abs(d[k].astype(np.float32))
        if not (np.isfinite(a).all() and ((a == 0) | (a >= 2.0 ** -30) & (a <= most)).all()): b.append("a value of " + k)
    if not ((d["p"] >= 0) & (d["p"] < T)).all(): b.append("an entry of p")
    none, least, most = [emit(mx_ref.quantize(np.full((128, 16), k, np.float32).astype(BF)))[1][0, 0] for k in (0.0, 2.0 ** -30, 2.0 ** 30)]
    for r in range(N):
        if ((d["wc"][r] == 0x7F) | (d["wc"][r] == 0xFF)).any(): b.append("wc: a code that is no number")
        s = mx_ref.live(d["ws"][r])
        if ((s != none) & ((s < least) | (s > most))).any(): b.append("ws: a scale out of range")
        a = np.abs(decode(pk(d["wc"][r], d["ws"][r])).astype(np.float64)).reshape(128, 512, 4)
        if not (np.sum(a, axis=(0, 2)) <= 32).all(): b.append("sizes in a column of W")
    return b
def order_of(t):
    place = np.argsort(np.argsort(T * t.reshape(-1) + np.arange(T))).reshape(8, C)
    o = np.argsort(place, axis=1)
    k = np.stack([np.searchsorted(place[g, o[g]], 8 * np.arange(C) + 7, side="right") for g in range(8)]) - 1
    k = np.maximum(k, 0)
    return place // 8, np.take_along_axis(o, k, axis=1), np.take_along_axis(o, np.minimum(k + 1, C - 1), axis=1)
def reference(x, u, v, p, wc, ws):
    qu = [mx_ref.quantize(u[r]) for r in range(N)]
    lay = [pk(wc[r], ws[r]) for r in range(N)]
    now = [x[r] for r in range(N)]
    pos = np.stack([gentries(p[r]) for r in range(N)]).astype(np.int64)
    for t in range(R):
        own, q = [], []
        for r in range(N):
            own.append(decode(mx_ref.quantize(now[r])).astype(BF))
            c, m, n = order_of(pos[r])
            z = ((gcols(own[r], m).astype(np.float32) + gcols(own[r], n).astype(np.float32)) * np.float32(0.5)).astype(BF)
            q.append(mx_ref.quantize(z))
            s = mx_ref.matmul(qu[r], q[r])[::16] + np.float32(0.0)
            step = np.argsort(np.argsort(s, axis=1, kind="stable"), axis=1)
            pos[r] += np.take_along_axis(step, c, axis=1)
        for r in range(N):
            came = pick(q[(r + N - 1) % N], np.arange(1, C, 2))
            h = tile([mx_ref.matmul(pick(lay[r], np.arange(128 * b, 128 * b + 128)), came) * np.float32(0.03125) for b in range(4)])
            c, m, n = order_of(pos[r])
            now[r] = (own[r].astype(np.float32) + gcols(h, c // 2).astype(np.float32)).astype(BF)
    y, pt = np.zeros((N, 128, C), np.float32), np.zeros((N, 8, C), np.float32)
    oc, osc = np.zeros((N, 128, 4 * C), np.uint8), np.zeros((N, 16, C), np.uint8)
    for r in range(N):
        q = mx_ref.quantize(now[r])
        y[r] = mx_ref.matmul(mx_ref.quantize(v[r]), q)
        pt[r] = pos[r]
        oc[r], osc[r] = emit(q)
    return {"y": y, "pt": pt, "oc": oc, "osc": osc}

from concourse.mybir import dt, AluOpType as A, ActivationFunctionType as F

C, R = 288, 3
K = 18
DOM = 3168
SIDE = 3200
SCOL = 7
SORD = 16
LOW = -144.0


def _sb(ty, **kw):
    return {k: ("sbuf", [128, n], ty) for k, n in kw.items()}


SCRATCH = {
    **_sb("bfloat16", xi=1152, ui=512, vi=512, ones=512, et=2048), **_sb("int32", pi=K),
    **_sb("float8_e4m3fn_x4", wq=512, uq=128, ur=128, vq=128, eq=512, qx=C), **_sb("uint8", wsc=512, usc=128, urs=128, vsc=128, esc=512, qxs=C),
    **_sb("int32", it=C, iq=C, qi=C, lk=K, gi=2), **_sb("float32", jj=C, dd=C, mf=C, kf=C, jf=C, jl=K, od=1, ev=1, ct=K, ip=DOM),
    **_sb("bfloat16", mb=C, gt=C, bm=C, b0=C, kb=C, jr=C, iw=C), **_sb("uint16", ex16=K, ul16=8),
    **_sb("float32", pl0=K, pl1=K, pl144=K, plm=K, kl=K, kr=C, pr=C, as_=K, s127=K, s3=K, sp=K, nr=K, cu=304, df=K, plf=K),
    **_sb("uint16", pl16=K, pu=C, sl16=K, ol16=K, xl16=36, c16=K, c216=K, pc16=K, k16=K, k116=K, o16=K), **_sb("int32", ci=K, c2i=K),
    **_sb("bfloat16", cb=4 * C, sc=K * 144, sc2=K * 144, junk=4 * C, vr=C, tab=3488, ctb=DOM, all=3216, ga=576, tr=576),
    **_sb("bfloat16", kw=2304, ks=1152, kx=C, ow=C, om=C, os2=C),
    **_sb("bfloat16", fh=1152, fs=1152, ff=576, gm=1152, zt=1152, tq=C, us=C, sg=4 * C, sr=C, sm=C, ss=C, hb=576, hg=576, xt=1152),
    **_sb("float32", rm=C, row=C, sl=C, uc=K, al=K, ar=K, ad=K, cn=K, yb=C), **_sb("uint16", st16=K),
    "pf": ("psum", [128, 2048], "float32"), "ph": ("psum", [128, 2048], "float32"),
}
for _r in range(R):
    SCRATCH.update(_sb("float8_e4m3fn_x4", **{"qz%d" % _r: C, "lc%d" % _r: 144}))
    SCRATCH.update(_sb("uint8", **{"qzs%d" % _r: C, "ls%d" % _r: 144}))
SEMAPHORES = ["V", "S", "P", "G", "ldp", "ldx", "ldu", "ldv", "ldw", "ex", "outs", "loc", "arr0", "arr1", "arr2"]


def rank_program(g, core, T, topo):
    rank = T.rank_of(core)
    if rank is None:
        return
    nxt = T.cores[(rank + 1) % len(T.cores)]
    queue = {"V": g.vector, "S": g.scalar, "P": g.tensor, "G": g, "Y": g.sync}
    total, seen = {}, {e: {} for e in queue}
    wrote, read = {}, {}

    def near(d, k):
        return [v for n, v in d.items() if n == k or n.startswith(k + ":") or k.startswith(n + ":")]

    def settle(e, rd, wr):
        need = {}
        for k in rd:
            for n in near(wrote, k):
                for s, v in n.items():
                    need[s] = max(need.get(s, 0), v)
        for k in wr:
            for n in near(wrote, k.rstrip("!")) + near(read, k.rstrip("!")):
                for s, v in n.items():
                    if s != e or k[-1] != "!":
                        need[s] = max(need.get(s, 0), v)
        for s in sorted(need):
            if seen[e].get(s, 0) < need[s]:
                queue[e].wait_ge(T.sem[s], need[s])
                seen[e][s] = need[s]

    def note(s, rd, wr):
        for d, ks in ((read, rd), (wrote, wr)):
            for k in ks:
                d.setdefault(k.rstrip("!"), {})[s] = total[s]

    def run(e, rd, wr, call):
        rd, wr = rd.split(), wr.split()
        settle(e, rd, wr)
        call().then_inc(T.sem[e], 1)
        total[e] = total.get(e, 0) + 1
        note(e, rd, wr)

    def dma(e, s, rd, wr, pairs):
        rd, wr = rd.split(), wr.split()
        settle(e, rd, wr)
        for o, i in pairs:
            queue[e].dma_start(o, i).then_inc(T.sem[s], 16)
            total[s] = total.get(s, 0) + 16
        note(s, rd, wr)

    def ts(rd, wr, out, in0, s1, op0, s2=None, op1=None):
        if op1 is None:
            run("V", rd, wr, lambda: g.vector.tensor_scalar(out=out, in0=in0, scalar1=s1, scalar2=None, op0=op0))
        else:
            run("V", rd, wr, lambda: g.vector.tensor_scalar(out=out, in0=in0, scalar1=s1, scalar2=s2, op0=op0, op1=op1))

    def tt(rd, wr, out, in0, in1, op):
        run("V", rd, wr, lambda: g.vector.tensor_tensor(out=out, in0=in0, in1=in1, op=op))

    def cp(rd, wr, out, in_):
        run("V", rd, wr, lambda: g.vector.tensor_copy(out, in_))

    def scan(rd, wr, out, d0, d1, init, op0, op1):
        run("V", rd, wr, lambda: g.vector.tensor_tensor_scan(out, d0, d1, init, op0, op1))

    def fill(wr, out, c):
        run("V", "", wr, lambda: g.vector.memset(out, c))

    def act(rd, wr, out, in_, func, **kw):
        run("S", rd, wr, lambda: g.scalar.activation(out, in_, func, **kw))

    def quant(rd, wr, q, s, t):
        run("V", rd, wr, lambda: g.vector.quantize_mx(q, s, t))

    def mx(rd, wr, out, a, asc, b, bsc):
        run("P", rd, wr, lambda: g.tensor.matmul_mx(out, a, asc, b, bsc, True, True))

    def iota(wr, out, pattern, base, cm, loose=False):
        if loose:
            run("G", "", wr, lambda: g.iota(out, pattern, base, cm, allow_small_or_imprecise_dtypes=True))
        else:
            run("G", "", wr, lambda: g.iota(out, pattern, base, cm))

    dma("Y", "ldp", "", "pi", [(T.pi[:], T.p[:])])
    dma("Y", "ldx", "", "xi", [(T.xi[:], T.x[:])])
    dma("Y", "ldu", "", "ui", [(T.ui[:], T.u[:])])
    dma("S", "ldw", "", "w", [(T.wq[:].bitcast(dt.uint8), T.wc[:]), (T.wsc[:], T.ws[:])])
    dma("S", "ldv", "", "vi", [(T.vi[:], T.v[:])])

    iota("ip:0", T.ip[:, 0:512], [[1, 512]], 0, 0, True)
    iota("iq", T.iq[:], [[0, C]], 0, 1)
    iota("lk", T.lk[:], [[16, K]], 0, 0)
    iota("jj", T.jj[:], [[1, C]], 0, 0, True)
    iota("it", T.it[:], [[0, K], [1, 16]], 0, 0)
    iota("all", T["all"][:], [[0, 3216]], int(LOW), 0, True)
    fill("ones", T.ones[:], 1.0)
    fill("tab", T.tab[:], LOW)
    fill("cu0", T.cu[:, 0:16], 0.0)
    fill("ct", T.ct[:], 127.0)
    for b in range(4):
        run("G", "ones", "et:%d" % b, lambda: g.affine_select(T.et[:, 512 * b:512 * b + 512], T.ones[:], [[-1, 512]], A.is_equal, 0.0, b, 4))
    act("ip:0", "ip:1", T.ip[:, 512:1024], T.ip[:, 0:512], F.Identity, bias=512.0)
    act("ip:0", "ip:2", T.ip[:, 1024:1536], T.ip[:, 0:512], F.Identity, bias=1024.0)
    ts("ip:0 ip:1", "ip:3", T.ip[:, 1536:2304], T.ip[:, 0:768], 1536.0, A.add)
    act("jj", "jf", T.jf[:], T.jj[:], F.Copy, scale=1.0 / 512)
    act("ip:0 ip:1", "ip:4", T.ip[:, 2304:3168], T.ip[:, 0:864], F.Identity, bias=2304.0)
    act("jj", "iw", T.iw[:], T.jj[:], F.Identity, bias=-143.0)
    act("jj", "jr", T.jr[:], T.jj[:], F.Identity, bias=-144.0)
    ts("iq", "qi", T.qi[:], T.iq[:], 15, A.bitwise_and)
    tt("qi lk", "jl", T.jl[:], T.qi[:, 0:K], T.lk[:], A.add)
    ts("jl", "jl", T.jl[:], T.jl[:], 1.0 / 512, A.mult)
    cp("pi", "pl0", T.pl0[:], T.pi[:])

    def constants2():
        ts("iq", "gi", T.gi[:], T.iq[:, 0:2], 4, A.logical_shift_right, 1, A.bitwise_and)
        cp("gi", "od", T.od[:], T.gi[:, 0:1])
        ts("od", "ev", T.ev[:], T.od[:], -1.0, A.mult, 1.0, A.add)

    def constants3():
        tt("qi it", "dd", T.dd[:], T.qi[:], T.it[:], A.subtract)
        cp("lk", "ul16", T.ul16[:], T.lk[:, 0:8])
        ts("dd", "mb", T.mb[:], T.dd[:], 0.0, A.is_equal)
        ts("it", "kb", T.kb[:], T.it[:], 0.0, A.is_gt)

    def constants4():
        ts("dd", "b0", T.b0[:], T.dd[:], 0.0, A.is_ge, 1024.0, A.mult)
        ts("b0", "bm", T.bm[:], T.b0[:], -512.0, A.add)

    def constants5():
        ts("dd", "mf", T.mf[:], T.dd[:], 0.0, A.is_equal)
        ts("it", "kf", T.kf[:], T.it[:], 0.0, A.is_gt)
        ts("dd", "gt", T.gt[:], T.dd[:], 0.0, A.is_lt)
        ts("lk", "ex16", T.ex16[:], T.lk[:], 15.0, A.add)
        ts("lk", "ct", T.ct[:, 0:SCOL], T.lk[:, 0:SCOL], 15.0, A.add)

    turn = {"cb": 0, "junk": 0, "sg": 0}

    def slot(name):
        turn[name] += 1
        n = turn[name] % 4
        return "%s:%d" % (name, n), C * n

    def counted(parts, out, rd, wr):
        key, o = slot("cb")
        for i, (a, b, row, sc, op) in enumerate(parts):
            if a < b:
                ts(rd, "%s:%d" % (key, i), T.cb[:, o + a:o + b], row[:, a:b], sc, op)
        return lambda: scan(key, wr, out, T.cb[:, o:o + 144], T.cb[:, o + 144:o + 288], -128.0, A.add, A.add)

    def staggered(jobs):
        last = None
        for j in jobs:
            now = counted(*j)
            if last:
                last()
            last = now
        last()

    def unpack():
        for b in range(4):
            mx("eq qx", "pf%d" % b, T.pf[:, 512 * b:512 * b + C], T.eq[:, 128 * b:128 * b + 128], T.esc[:, 128 * b:128 * b + 128], T.qx[:], T.qxs[:])
        for b in range(4):
            act("pf%d" % b, "fh:%d pf%d!" % (b, b), T.fh[:, C * b:C * b + C], T.pf[:, 512 * b:512 * b + C], F.Copy, scale=0.5)
            act("fh:%d o16" % b, "fs:%d" % b, T.fs[:, C * b:C * b + C], T.fh[:, C * b:C * b + C].indirect(T.o16[:]), F.Copy)

    def order(pl, r, last):
        PL = T[pl]
        dom = 2304 + 288 * (r + 1)
        cp(pl, "pl16", T.pl16[:], PL[:])
        tt(pl + " jl", "kl", T.kl[:], PL[:], T.jl[:], A.add)
        tt("ip pl16 jf", "kr", T.kr[:], T.ip[:].indirect(T.pl16[:]), T.jf[:], A.add)
        cp("ip pl16", "pu", T.pu[:], T.ip[:].indirect(T.pl16[:]))
        for k in range(SORD):
            key, o = slot("junk")
            act("kr kl", "as:%d %s" % (k, key), T.junk[:, o:o + C], T.kr[:], F.Sign, scale=-1.0, bias=T.kl[:, k:k + 1], accum_out=T.as_[:, k:k + 1])
        staggered([([(0, C, T.kr, T.kl[:, k:k + 1], A.is_lt)], T.sc2[:, 144 * k:144 * k + 144], "kr kl", "sc2:%d" % k) for k in range(SORD, K)] +
                  [([(0, C, T.pu, PL[:, k:k + 1], A.is_le)], T.sc[:, 144 * k:144 * k + 144], "pu " + pl, "sc:%d" % k) for k in range(K)])
        if r < 0:
            constants2()
        ts("sc2", "as:v", T.as_[:, SORD:K], T.sc2[:, 144 * SORD + 143:144 * K:144], 2.0, A.mult, 256.0 - 287.0, A.add)
        ts("as", "sl16", T.sl16[:], T.as_[:], 0.5, A.mult, 143.5, A.add)
        ts("as", "s127", T.s127[:], T.as_[:], 0.5, A.mult, 16.5, A.add)
        ts("as", "s3", T.s3[:], T.as_[:], 0.5, A.mult, 143.5 + SIDE, A.add)
        act("iw sl16", "vr", T.vr[:], T.iw[:].indirect(T.sl16[:]), F.Copy)
        tt("sc s127", "nr", T.nr[:], T.sc[:, 143:144 * K:144], T.s127[:], A.is_gt)
        tt("nr s3", "nr", T.nr[:], T.nr[:], T.s3[:], A.mult)
        tt("nr " + pl, "nr", T.nr[:], T.nr[:], PL[:], A.max)
        cp("nr", "ol16", T.ol16[:], T.nr[:])
        cp("vr ol16", "tab", T.tab[:].indirect(T.ol16[:]), T.vr[:])
        scan("tab", "ctb", T.ctb[:, 0:dom], T.tab[:, 0:dom], T.tab[:, 0:dom], LOW, A.max, A.max)
        if not last:
            iota("tab", T.tab[:, 0:DOM], [[0, DOM]], int(LOW), 0, True)
        if r < 0:
            act("all", "kw", T.kw[:], T["all"][:, 0:2304], F.Copy)
        if last:
            act("ip pl16", "pr", T.pr[:], T.ip[:].indirect(T.pl16[:]), F.Copy)
            dma("Y", "outs", "pr", "", [(T.pt[:], T.pr[0:128:16, :])])
        if r >= 0:
            for b in range(4):
                mx("w land%d" % r, "ph%d" % b, T.ph[:, 512 * b:512 * b + 144], T.wq[:, 128 * b:128 * b + 128], T.wsc[:, 128 * b:128 * b + 128], T["lc%d" % r][:], T["ls%d" % r][:])
            for b in range(4):
                act("ph%d" % b, "hb:%d ph%d!" % (b, b), T.hb[:, 144 * b:144 * b + 144], T.ph[:, 512 * b:512 * b + 144], F.Copy, scale=0.03125)
        up = [(T["all"][16 * (h + 1) + h:128:16, 0:dom], T.ctb[16 * h:16 * h + 7 - h, 0:dom]) for h in range(7)]
        dn = [(T["all"][h:16 * h:16, 1:dom + 1], T.ctb[16 * h + 8:16 * h + 8 + h, 0:dom]) for h in range(1, 8)]
        settle("S", ["ctb"], ["all"])
        dma("Y", "ex", "ctb", "all", up)
        dma("S", "ex", "ctb", "alls", dn)
        note("ex", ["ctb"], ["all"])
        ts(pl, "plm", T.plm[:], PL[:], -float(SIDE), A.add)
        ts("s127", "sp", T.sp[:], T.s127[:], 127.0 + 4608.0, A.add)
        ts("plm ev", "xl16:0", T.xl16[:, 0:36:2], T.plm[:], T.ev[:], A.mult, float(SIDE), A.add)
        ts("plm od", "xl16:1", T.xl16[:, 1:36:2], T.plm[:], T.od[:], A.mult, float(SIDE), A.add)
        if r < 0:
            constants3()
            quant("xi", "qx", T.qx[:], T.qxs[:], T.xi[:])
        if not last:
            cp("jr sl16", "ow", T.ow[:].indirect(T.sl16[:]), T.jr[:])
            tt("ow mb", "om", T.om[:], T.ow[:], T.mb[:], A.mult)
            scan("kb om", "os2", T.os2[:], T.kb[:], T.om[:], 0.0, A.mult, A.add)
            ts("os2", "o16", T.o16[:], T.os2[:, 15:C:16], 144.0, A.add)
            ts(pl, "pl144", T.pl144[:], PL[:], 144.0, A.add)
        act("all xl16", "ga:0", T.ga[:, 0:C], T["all"][:].indirect(T.xl16[:, 0:K]), F.Copy)
        cp("all xl16", "ga:1", T.ga[:, C:2 * C], T["all"][:].indirect(T.xl16[:, K:2 * K]))
        if r < 0:
            quant("et", "eq", T.eq[:], T.esc[:], T.et[:])
            unpack()
        run("V", "ga", "tr", lambda: g.vector.transpose(T.tr[:], T.ga[:]))
        scan("tr", "cu", T.cu[:, 16:304], T.tr[:, 0:576:2], T.tr[:, 1:576:2], 0.0, A.add, A.add)
        tt("cu cu0", "df", T.df[:], T.cu[:, 31:304:16], T.cu[:, 15:288:16], A.subtract)
        tt("df sp", "plf", T.plf[:], T.df[:], T.sp[:], A.add)
        if r >= 0:
            ts("plf", "c2i", T.c2i[:], T.plf[:], 0.0625, A.mult, -0.46875, A.add)
        if not last:
            ts("plf", "ci", T.ci[:], T.plf[:], 0.125, A.mult, -0.4375, A.add)
            cp("plf", "pc16", T.pc16[:], T.plf[:])
        if r >= 0:
            cp("c2i", "c216", T.c216[:], T.c2i[:])
        if not last:
            cp("ci", "c16", T.c16[:], T.ci[:])

    def deal():
        for b in (2, 3):
            act("hb c216", "hg:%d" % b, T.hg[:, C * b - 576:C * b - C], T.hb[:, 144 * b:144 * b + 144].indirect(T.c216[:]), F.Copy)
        for b in (0, 1):
            tt("hb c216 ff:%d" % b, "xt:%d" % b, T.xt[:, b:1152:4], T.hb[:, 144 * b:144 * b + 144].indirect(T.c216[:]), T.ff[:, C * b:C * b + C], A.add)
        for b in (2, 3):
            tt("hg:%d pf%d" % (b, b), "xt:%d pf%d!" % (b, b), T.xt[:, b:1152:4], T.hg[:, C * b - 576:C * b - C], T.pf[:, 512 * b:512 * b + C], A.add)
        quant("xt", "qx", T.qx[:], T.qxs[:], T.xt[:])

    def lists():
        cp("vr pc16", "kw", T.kw[:].indirect(T.pc16[:]), T.vr[:])
        scan("kw", "ks", T.ks[:], T.kw[:, 0:2304:2], T.kw[:, 1:2304:2], -143.0, A.max, A.max)
        scan("bm ks", "kx:0", T.kx[:, 0:144], T.bm[:, 0:144], T.ks[:, 7:1152:8], 0.0, A.max, A.min)
        scan("bm ks", "kx:1", T.kx[:, 144:288], T.bm[:, 0:144], T.ks[:, 3:1152:8], 0.0, A.max, A.min)
        ts("kx", "k16", T.k16[:], T.kx[:, 15:C:16], 143.0, A.add)
        ts("kx", "k116", T.k116[:], T.kx[:, 15:C:16], 144.0, A.add, 287.0, A.min)

    def join(r):
        qz, qs = T["qz%d" % r], T["qzs%d" % r]
        for b in (2, 3):
            act("fs:%d k16" % b, "gm:%d" % b, T.gm[:, C * b:C * b + C], T.fs[:, C * b:C * b + C].indirect(T.k16[:]), F.Copy)
        for b in (0, 1):
            cp("fs:%d k16" % b, "gm:%d" % b, T.gm[:, C * b:C * b + C], T.fs[:, C * b:C * b + C].indirect(T.k16[:]))
        for b in range(4):
            tt("fs:%d k116 gm:%d" % (b, b), "zt:%d" % b, T.zt[:, b:1152:4], T.fs[:, C * b:C * b + C].indirect(T.k116[:]), T.gm[:, C * b:C * b + C], A.add)
        quant("zt", "qz%d" % r, qz[:], qs[:], T.zt[:])
        rid, pid = topo.addr(nxt, core)
        eng = topo.mask(core, nxt)
        n = len(topo.engines(core, nxt))
        settle("G", ["qz%d" % r], [])
        arr = "arr%d" % r
        g.remote_dma(T["lc%d" % r][:].bitcast(dt.uint8), qz[:, 0:144].bitcast(dt.uint8), T.sem[arr], T.sem.loc, pid, rid, eng)
        g.remote_dma(T["ls%d" % r][:], qs[:, 0:144], T.sem[arr], T.sem.loc, pid, rid, eng)
        total[arr] = 2 * n
        total["loc"] = total.get("loc", 0) + 2 * n
        note(arr, [], ["land%d" % r])
        if r < R - 1:
            iota("kw", T.kw[:], [[0, 2304]], int(LOW), 0, True)
        for b in (0, 1):
            act("pf%d" % b, "ff:%d pf%d!" % (b, b), T.ff[:, C * b:C * b + C], T.pf[:, 512 * b:512 * b + C], F.Copy)

    def move(r, pl, new):
        qz, qs = T["qz%d" % r], T["qzs%d" % r]
        pv = T.ph
        mx("ur qz%d" % r, "ph3", pv[:, 1536:1536 + C], T.ur[:], T.urs[:], qz[:], qs[:])
        tt("ph3 mf", "rm:1 ph3!", T.rm[:, 1:C:2], pv[:, 1536:1680], T.mf[:, 1:C:2], A.mult)
        tt("ph3 mf", "rm:0 ph3!", T.rm[:, 0:C:2], pv[:, 1680:1824], T.mf[:, 0:C:2], A.mult)
        act("ph3", "row:1 ph3!", T.row[:, 1:C:2], pv[:, 1536:1680], F.Copy)
        act("ph3", "row:0 ph3!", T.row[:, 0:C:2], pv[:, 1680:1824], F.Copy)
        scan("kf rm", "sl", T.sl[:], T.kf[:], T.rm[:], 0.0, A.mult, A.add)
        late = None
        for k in range(SCOL):
            e = 16 * k + 16
            key, o = slot("sg")
            act("row sl", key, T.sg[:, o:o + C], T.row[:], F.Sign, scale=-1.0, bias=T.sl[:, 16 * k + 15:16 * k + 16])
            if late:
                late()

            def late(k=k, e=e, o=o, key=key):
                jk, j = slot("junk")
                act(key, "al:%d %s:0" % (k, jk), T.junk[:, j:j + e], T.sg[:, o:o + e], F.Relu, scale=-1.0, accum_out=T.al[:, k:k + 1])
                act(key, "ar:%d %s:1" % (k, jk), T.junk[:, j + e:j + C], T.sg[:, o + e:o + C], F.Relu, accum_out=T.ar[:, k:k + 1])
        late()
        staggered([([(0, 16 * k + 16, T.row, T.sl[:, 16 * k + 15:16 * k + 16], A.is_le), (16 * k + 16, C, T.row, T.sl[:, 16 * k + 15:16 * k + 16], A.is_lt)],
                    T.sc[:, 144 * k:144 * k + 144], "row sl", "sc:%d" % k) for k in range(SCOL, K)])
        tt("sl ex16 row", "tq", T.tq[:], T.sl[:].indirect(T.ex16[:]), T.row[:], A.is_equal)
        scan("tq gt", "us", T.us[:], T.tq[:], T.gt[:], 0.0, A.add, A.mult)
        tt("us ct", "uc", T.uc[:], T.us[:, 15:C:16], T.ct[:], A.subtract)
        tt("al ar", "ad", T.ad[:, 0:SCOL], T.ar[:, 0:SCOL], T.al[:, 0:SCOL], A.subtract)
        tt("sc uc", "cn:1", T.cn[:, SCOL:K], T.sc[:, 144 * SCOL + 143:144 * K:144], T.uc[:, SCOL:K], A.subtract)
        tt("ad uc", "cn:0", T.cn[:, 0:SCOL], T.ad[:, 0:SCOL], T.uc[:, 0:SCOL], A.subtract)
        cp("cn", "st16", T.st16[:], T.cn[:])
        act("jr st16", "sr", T.sr[:], T.jr[:].indirect(T.st16[:]), F.Copy)
        tt("sr c16 mb", "sm", T.sm[:], T.sr[:].indirect(T.c16[:]), T.mb[:], A.mult)
        scan("kb sm", "ss", T.ss[:], T.kb[:], T.sm[:], 0.0, A.mult, A.add)
        tt("pl144 ss", new, T[new][:], T.pl144[:], T.ss[:, 15:C:16], A.add)

    order("pl0", -1, False)
    constants4()
    lists()
    quant("ui", "uq", T.uq[:], T.usc[:], T.ui[:])
    cp("uq ul16", "ur:0", T.ur[:, 0:128].bitcast(dt.uint32), T.uq[:, 0:128].bitcast(dt.uint32).indirect(T.ul16[:, 0:8]))
    cp("uq ul16", "ur:1", T.urs[:, 0:128], T.usc[:, 0:128].indirect(T.ul16[:, 0:8]))
    constants5()
    for r in range(R):
        pl, new = ("pl0", "pl1") if r % 2 == 0 else ("pl1", "pl0")
        join(r)
        move(r, pl, new)
        order(new, r, r == R - 1)
        deal()
        if r < R - 1:
            unpack()
            lists()
    dma("Y", "outs", "qx", "", [(T.oc[:], T.qx[:].bitcast(dt.uint8))] + [(T.osc[4 * k:4 * k + 4, :], T.qxs[32 * k:32 * k + 4, :]) for k in range(4)])
    quant("vi", "vq", T.vq[:], T.vsc[:], T.vi[:])
    mx("vq qx", "ph0", T.ph[:, 0:C], T.vq[:], T.vsc[:], T.qx[:], T.qxs[:])
    act("ph0", "yb ph0!", T.yb[:], T.ph[:, 0:C], F.Copy)
    dma("S", "outs", "yb", "", [(T.y[:], T.yb[:])])
    for s in sorted(total):
        if seen["G"].get(s, 0) < total[s]:
            g.wait_ge(T.sem[s], total[s])
